import numpy as np
import ml_dtypes


def mxq(x, axis, fmt="e4m3"):
    dtype, down = {"e4m3": (ml_dtypes.float8_e4m3fn, 7), "e5m2": (ml_dtypes.float8_e5m2, 14)}[fmt]
    v = np.moveaxis(np.asarray(x, np.float32).astype(ml_dtypes.bfloat16).astype(np.float64), axis, -1)
    blocks = v.reshape(v.shape[:-1] + (-1, 32))
    amax = np.abs(blocks).max(-1, keepdims=True)
    byte = np.maximum(np.where(amax > 0, np.frexp(amax)[1] - 1 + 127, 0) - down, 1)
    scale = np.exp2(byte - 127.0)
    codes = (blocks / scale).astype(np.float32).astype(dtype).astype(np.float64)
    return np.moveaxis((codes * scale).reshape(v.shape), -1, axis)


WIDE = False


def mx_kscale(k):
    if not WIDE:
        return np.ones(k)
    levels = np.array([10, -10, 5, -5, 0])
    if k % 512:
        return np.exp2(np.random.permutation(np.resize(levels, k // 32))).repeat(32)
    a = np.empty((k // 512, 16))
    for p in range(k // 512):
        a[p, :8] = np.random.permutation(np.resize(levels, 8))
        for g in range(8):
            far = levels[np.abs(levels - a[p, g]) >= 10]
            a[p, g + 8] = far[np.random.randint(len(far))]
    return np.exp2(a.ravel()).repeat(32)


BF16 = ml_dtypes.bfloat16


def bf(x):
    return np.asarray(x, np.float32).astype(BF16)


def f64(x):
    return np.asarray(x).astype(np.float64)


E2M1 = np.array([0.0, 0.5, 1.0, 1.5, 2.0, 3.0, 4.0, 6.0, -0.0, -0.5, -1.0, -1.5, -2.0, -3.0, -4.0, -6.0])


def pack_weight(w, fmt):
    k, n = w.shape
    w = f64(bf(w)).reshape(k // 32, 32, n)
    amax = np.abs(w).max(1)
    if fmt == "e4m3":
        byte = np.frexp(amax)[1] - 1 + 127 - 7
    else:
        mant, ex = np.frexp(amax / 6.0)
        byte = np.where(mant > 0.5, ex, ex - 1) + 127
    byte = np.clip(np.where(amax > 0, byte, 1), 1, 254)
    scaled = (w * np.exp2(127.0 - byte)[:, None, :]).reshape(k, n).astype(np.float32)
    by_word = np.ascontiguousarray(scaled.reshape(k // 512, 128, 4, n).transpose(0, 1, 3, 2))
    if fmt == "e4m3":
        words = by_word.astype(ml_dtypes.float8_e4m3fn).view(np.uint8)
    else:
        c = by_word.astype(ml_dtypes.float4_e2m1fn).view(np.uint8) & 0xF
        words = c[..., 0::2] | (c[..., 1::2] << 4)
    return np.ascontiguousarray(words), np.ascontiguousarray(byte.astype(np.uint8).reshape(k // 512, 16, n))


def unpack_weight(words, scales, fmt):
    g, p, n, _ = words.shape
    if fmt == "e4m3":
        vals = np.ascontiguousarray(words).view(ml_dtypes.float8_e4m3fn).astype(np.float64)
    else:
        nib = np.empty((g, p, n, 4), np.uint8)
        nib[..., 0::2] = words & 0xF
        nib[..., 1::2] = words >> 4
        vals = E2M1[nib]
    vals = vals * np.repeat(np.exp2(scales.astype(np.float64) - 127.0), 8, axis=1)[..., None]
    return vals.transpose(0, 1, 3, 2).reshape(g * 512, n)
def pack4(w):
    words, scales = pack_weight(w, "e2m1")
    return words.reshape(words.shape[0], 128, -1), scales


def unpack4(words, scales):
    return unpack_weight(words.reshape(words.shape[0], 128, -1, 2), scales, "e2m1")


M, K, H, D, E, R = 1024, 1536, 4, 512, 128, 512
BASE = 10000.0


def draw0():
    s = mx_kscale(K)
    t = mx_kscale(D)
    size = np.exp(0.3 * np.random.standard_normal((M, 1)))
    c_q = np.random.standard_normal((M, K)) * size * s
    uq = np.random.standard_normal((K, H * (D + E))) / np.sqrt(K) / s[:, None]
    uk = np.random.standard_normal((H, D, R)) / np.sqrt(D) / t[:, None]
    uq_words, uq_scales = pack4(uq)
    uk_words, uk_scales = pack_weight(uk.reshape(H * D, R), "e4m3")
    position = np.random.uniform(0.0, BASE, (M, 1))
    angle = position * BASE ** (-np.arange(E // 2) / (E // 2))
    return {"c_q": bf(c_q),
            "uq_words": uq_words,
            "uq_scales": uq_scales,
            "b_q": bf(0.3 * np.random.standard_normal(H * (D + E))),
            "g_nope": bf((1 + 0.1 * np.random.standard_normal(D)) * t),
            "g_rope": bf(1 + 0.1 * np.random.standard_normal(E)),
            "rot_cos": bf(np.cos(angle)),
            "rot_sin": bf(np.sin(angle)),
            "uk_words": uk_words,
            "uk_scales": uk_scales,
            "g_kv": bf(1 + 0.1 * np.random.standard_normal(R))}


def core(c_q, uq_words, uq_scales, b_q, g_nope, g_rope, rot_cos, rot_sin, uk_words, uk_scales, g_kv):
    y = (mxq(f64(c_q), 1, "e4m3") @ unpack4(uq_words, uq_scales)) + f64(b_q)
    y = y.reshape(M, H, D + E)
    y = y / np.sqrt(np.mean(y * y, axis=2, keepdims=True))
    nope = y[:, :, :D] * f64(g_nope)
    rope = y[:, :, D:] * f64(g_rope)
    uk = unpack_weight(uk_words, uk_scales, "e4m3")
    lat = mxq(nope, 2, "e4m3").transpose(1, 0, 2) @ uk.reshape(H, D, R)
    lat = lat * f64(g_kv)
    a, b = rope[:, :, :E // 2], rope[:, :, E // 2:]
    c, d = f64(rot_cos)[:, None, :], f64(rot_sin)[:, None, :]
    rot = np.concatenate([a * c - b * d, a * d + b * c], axis=2).transpose(1, 0, 2)
    return lat, rot


def e4m3fn_bytes(y):
    return np.clip(np.asarray(y, np.float64), -448.0, 448.0).astype(np.float32).astype(ml_dtypes.float8_e4m3fn).view(np.uint8)


def e4m3fn_values(b):
    return np.asarray(b, np.uint8).view(ml_dtypes.float8_e4m3fn).astype(np.float64)


def setup_inputs():
    d = draw0()
    x0 = np.asarray(d['c_q']).astype(np.float64)
    s = (np.max(np.abs(x0), axis=(0,), keepdims=True) / 448.0).astype(np.float32)
    out = {}
    for k, v in d.items():
        if k == 'c_q':
            out['c_q_bytes'] = e4m3fn_bytes(x0 / s.astype(np.float64))
            out['c_q_scale'] = s
        else:
            out[k] = v
    return out


def reference(c_q_bytes, c_q_scale, uq_words, uq_scales, b_q, g_nope, g_rope, rot_cos, rot_sin, uk_words, uk_scales, g_kv):
    return core(e4m3fn_values(c_q_bytes) * c_q_scale.astype(np.float64), uq_words, uq_scales, b_q, g_nope, g_rope, rot_cos, rot_sin, uk_words, uk_scales, g_kv)

@@ -1,0 +1,308 @@
+from contextlib import ExitStack
+
+import concourse.mybir as mybir
+from concourse.masks import make_identity
+
+M, K, H, D, E, R = 1024, 1536, 4, 512, 128, 512
+FLOPS = 2 * M * K * H * (D + E) + 2 * H * M * D * R
+
+F32 = mybir.dt.float32
+BF16 = mybir.dt.bfloat16
+U32 = mybir.dt.uint32
+I32 = mybir.dt.int32
+U8 = mybir.dt.uint8
+FP8 = mybir.dt.float8_e4m3fn
+FP8X4 = mybir.dt.float8_e4m3fn_x4
+FP4X4 = mybir.dt.float4_e2m1fn_x4
+ALU = mybir.AluOpType
+ACT = mybir.ActivationFunctionType
+
+P = 128
+TILES = M // P
+PASSES = K // 512
+HEAD = D + E
+WIDTH = H * HEAD
+BANK = 512
+BANKS = WIDTH // BANK
+HALF = E // 2
+S_HEADS = 3
+
+
+def tile_mla_absorbed_query_f7_kernel(tc, c_q_bytes, c_q_scale, uq_words, uq_scales, b_q, g_nope, g_rope,
+                                                  rot_cos, rot_sin, uk_words, uk_scales, g_kv, lat_out, rot_out):
+    nc = tc.nc
+    with ExitStack() as ctx:
+        keep = ctx.enter_context(tc.tile_pool(name="keep", bufs=1))
+        work = ctx.enter_context(tc.tile_pool(name="work", bufs=2))
+        psum = ctx.enter_context(tc.psum_pool(name="psum", bufs=2))
+        ctx.enter_context(tc.manual_schedule())
+
+        xb = [keep.tile([P, K], U8, name="xb%d" % i) for i in range(TILES)]
+        cs = keep.tile([P, PASSES, 4], F32, name="cs")
+        uqw = [keep.tile([P, PASSES, 2 * BANK], U8, name="uqw%d" % b, align_bytes=64) for b in range(BANKS)]
+        uqs = keep.tile([P, PASSES, WIDTH], U8, name="uqs", align_bytes=64)
+        ukw = [keep.tile([P, 4 * R], U8, name="ukw%d" % h, align_bytes=64) for h in range(H)]
+        uks = keep.tile([P, R], U8, name="uks", align_bytes=64)
+        bias = keep.tile([P, WIDTH], BF16, name="bias")
+        gn = keep.tile([P, D], BF16, name="gn")
+        gr = keep.tile([P, E], BF16, name="gr")
+        gkv = keep.tile([P, R], BF16, name="gkv")
+        cos = keep.tile([P, TILES, HALF], BF16, name="cos")
+        sin = keep.tile([P, TILES, HALF], BF16, name="sin")
+        t1 = keep.tile([P, TILES, E], F32, name="t1")
+        t2 = keep.tile([P, TILES, E], F32, name="t2")
+        ngr = keep.tile([P, HALF], F32, name="ngr")
+        ident = keep.tile([P, P], F32, name="ident")
+        warm = keep.tile([P, 1], F32, name="warm")
+
+        def load_x(i):
+            nc.sync.dma_start(out=xb[i][:], in_=c_q_bytes[i * P:(i + 1) * P, :])
+
+        nc.vector.memset(uqs[:].rearrange("p g n -> p (g n)").bitcast(I32), 0)
+        nc.vector.memset(uks[:].bitcast(I32), 0)
+        nc.vector.memset(warm[:], 1.0)
+        nc.scalar.dma_start(out=cs[:], in_=c_q_scale.rearrange("o (g p t) -> p (o g) t", p=P, t=4))
+        nc.scalar.activation(out=warm[:], in_=warm[:], func=ACT.Abs_reciprocal_sqrt)
+        make_identity(nc, ident[:])
+        load_x(0)
+        load_x(1)
+        for q in range(4):
+            nc.sync.dma_start(out=uqs[32 * q:32 * q + 4, :, :].bitcast(I32),
+                              in_=uq_scales[:, 4 * q:4 * q + 4, :].rearrange("g r n -> r g n").bitcast(I32))
+
+        def load_uq(b):
+            nc.sync.dma_start(out=uqw[b][:],
+                              in_=uq_words[:, :, 2 * BANK * b:2 * BANK * (b + 1)].rearrange("g p n -> p g n"))
+
+        load_uq(0)
+        nc.sync.dma_start(out=bias[:], in_=b_q.partition_broadcast(P))
+        load_uq(1)
+        nc.sync.dma_start(out=gn[:], in_=g_nope.partition_broadcast(P))
+        for b in range(2, BANKS):
+            load_uq(b)
+        nc.scalar.dma_start(out=gr[:], in_=g_rope.partition_broadcast(P))
+        nc.scalar.dma_start(out=cos[:], in_=rot_cos.rearrange("(i p) j -> p i j", p=P))
+        nc.scalar.dma_start(out=sin[:], in_=rot_sin.rearrange("(i p) j -> p i j", p=P))
+        load_x(2)
+        for q in range(4):
+            nc.sync.dma_start(out=uks[32 * q:32 * q + 16, :].bitcast(I32),
+                              in_=uk_scales[:, 4 * q:4 * q + 4, :].bitcast(I32))
+        for h in range(H):
+            nc.sync.dma_start(out=ukw[h][:].bitcast(I32),
+                              in_=uk_words[h].rearrange("p n t -> p (n t)").bitcast(I32))
+        nc.sync.dma_start(out=gkv[:], in_=g_kv.partition_broadcast(P))
+        for i in range(3, TILES):
+            load_x(i)
+
+        def gain(col):
+            return gr[:, col:col + HALF].unsqueeze(1).to_broadcast([P, TILES, HALF])
+
+        nc.gpsimd.tensor_scalar(out=ngr[:], in0=gr[:, HALF:E], scalar1=-1.0, scalar2=None, op0=ALU.mult)
+        nc.gpsimd.tensor_tensor(out=t1[:, :, 0:HALF], in0=cos[:], in1=gain(0), op=ALU.mult)
+        nc.gpsimd.tensor_tensor(out=t1[:, :, HALF:E], in0=cos[:], in1=gain(HALF), op=ALU.mult)
+        nc.gpsimd.tensor_tensor(out=t2[:, :, 0:HALF], in0=sin[:],
+                                in1=ngr[:].unsqueeze(1).to_broadcast([P, TILES, HALF]), op=ALU.mult)
+        nc.gpsimd.tensor_tensor(out=t2[:, :, HALF:E], in0=sin[:], in1=gain(0), op=ALU.mult)
+
+        xw, xt, xg, xc, xs = {}, {}, {}, {}, {}
+        acc, y, yg, ss, rinv, nope = {}, {}, {}, {}, {}, {}
+        nt, ng, ncd, nsc = {}, {}, {}, {}
+        lacc, lat, rsum = {}, {}, {}
+
+        def cast(i):
+            t = work.tile([P, K], BF16, name="xw", bufs=3)
+            nc.scalar.copy(out=t[:], in_=xb[i][:].bitcast(FP8))
+            xw[i] = t
+
+        def x_turn(i):
+            words = xw[i][:].bitcast(F32)
+            for g in range(PASSES):
+                if g % 2 == 0:
+                    bank = psum.tile([P, 4, P], F32, name="turn", bufs=3)
+                for u in range(2):
+                    nc.tensor.transpose(bank[:, 2 * (g % 2) + u, :], words[:, 256 * g + u:256 * (g + 1):2], ident[:])
+                xt[i, g] = bank[:, 2 * (g % 2):2 * (g % 2) + 2, :]
+
+        def x_scale(i):
+            t = work.tile([P, PASSES, 4 * P], BF16, name="xg", align_bytes=64)
+            for g in range(PASSES):
+                nc.vector.tensor_tensor(
+                    out=t[:, g, :].rearrange("p (r u e) -> p r u e", u=2, e=2),
+                    in0=xt[i, g].bitcast(BF16).rearrange("p u (r e) -> p r u e", e=2),
+                    in1=cs[:, g, :].rearrange("p (u e) -> p u e", u=2).unsqueeze(1).to_broadcast([P, P, 2, 2]),
+                    op=ALU.mult)
+            xg[i] = t
+
+        def x_quant(i):
+            codes = work.tile([P, PASSES, P], U32, name="xc", align_bytes=64)
+            scales = work.tile([P, PASSES, P], U8, name="xs", align_bytes=64)
+            for a, b in ((0, 2), (2, 3)):
+                nc.vector.quantize_mx(out=codes[:, a:b, :].rearrange("p g n -> p (g n)").bitcast(FP8X4),
+                                      scales=scales[:, a:b, :].rearrange("p g n -> p (g n)"),
+                                      in_=xg[i][:, a:b, :].rearrange("p g n -> p (g n)"))
+            xc[i], xs[i] = codes, scales
+
+        def up(i, b):
+            t = psum.tile([P, BANK], F32, name="acc", bufs=5)
+            for g in range(PASSES):
+                nc.tensor.matmul_mx(out=t[:], lhsT=xc[i][:, g, :].bitcast(FP8X4), lhsT_scale=xs[i][:, g, :],
+                                    rhs=uqw[b][:, g, :].bitcast(FP4X4), rhs_scale=uqs[:, g, BANK * b:BANK * (b + 1)],
+                                    start=(g == 0), stop=(g == PASSES - 1))
+            acc[i, b] = t
+
+        def add_bias(i, b):
+            if b == 0:
+                t = work.tile([P, WIDTH], F32, name="y", bufs=3)
+                y[i] = t
+            cols = slice(BANK * b, BANK * (b + 1))
+            nc.vector.tensor_tensor(out=y[i][:, cols], in0=acc[i, b][:], in1=bias[:, cols], op=ALU.add)
+
+        def square(i, h):
+            if h == 0:
+                t = work.tile([P, H], F32, name="ss")
+                ss[i] = t
+            junk = work.tile([P, HEAD], BF16, name="junk")
+            nc.scalar.activation(out=junk[:], in_=y[i][:, HEAD * h:HEAD * (h + 1)], func=ACT.Square,
+                                 accum_out=ss[i][:, h:h + 1])
+
+        def root(i):
+            t = work.tile([P, H], F32, name="rinv", bufs=3)
+            nc.scalar.activation(out=t[:], in_=ss[i][:], func=ACT.Abs_reciprocal_sqrt, scale=1.0 / HEAD)
+            rinv[i] = t
+
+        def gain_nope(i, h):
+            t = work.tile([P, D], F32, name="yg%d" % h)
+            nc.gpsimd.tensor_tensor(out=t[:], in0=y[i][:, HEAD * h:HEAD * h + D], in1=gn[:], op=ALU.mult)
+            yg[i, h] = t
+
+        def norm_s(i, h):
+            t = work.tile([P, D], BF16, name="nope%d" % h)
+            nc.scalar.activation(out=t[:].rearrange("p (u q e) -> p u q e", u=2, e=2),
+                                 in_=yg[i, h][:].rearrange("p (q u e) -> p u q e", u=2, e=2),
+                                 func=ACT.Copy, scale=rinv[i][:, h:h + 1])
+            nope[i, h] = t
+
+        def norm_v(i, h):
+            t = work.tile([P, D], BF16, name="nope%d" % h)
+            part = y[i][:, HEAD * h:HEAD * h + D].rearrange("p (q u e) -> p u q e", u=2, e=2)
+            gpart = gn[:].rearrange("p (q u e) -> p u q e", u=2, e=2)
+            for u in range(2):
+                nc.vector.scalar_tensor_tensor(out=t[:, u * 256:(u + 1) * 256].rearrange("p (q e) -> p q e", e=2),
+                                               in0=part[:, u], scalar=rinv[i][:, h:h + 1], in1=gpart[:, u],
+                                               op0=ALU.mult, op1=ALU.mult)
+            nope[i, h] = t
+
+        def nope_turn(i, k):
+            bank = psum.tile([P, 4, P], F32, name="turn", bufs=3)
+            for j in range(2):
+                words = nope[i, 2 * k + j][:].bitcast(F32)
+                for u in range(2):
+                    nc.tensor.transpose(bank[:, 2 * j + u, :], words[:, P * u:P * (u + 1)], ident[:])
+            nt[i, k] = bank
+
+        def nope_out(i, k):
+            t = work.tile([P, 1024], BF16, name="ng", bufs=3, align_bytes=64)
+            nc.scalar.copy(out=t[:].bitcast(F32).rearrange("p (h r u) -> p h r u", h=2, u=2),
+                           in_=nt[i, k][:].rearrange("p (h u) r -> p h r u", h=2))
+            ng[i, k] = t
+
+        def nope_quant(i, k):
+            codes = work.tile([P, 256], U32, name="ncd", bufs=4, align_bytes=64)
+            scales = work.tile([P, 256], U8, name="nsc", bufs=4, align_bytes=64)
+            nc.vector.quantize_mx(out=codes[:].bitcast(FP8X4), scales=scales[:], in_=ng[i, k][:])
+            ncd[i, k], nsc[i, k] = codes, scales
+
+        def absorb(i, h):
+            t = psum.tile([P, BANK], F32, name="acc", bufs=5)
+            cols = slice(P * (h % 2), P * (h % 2 + 1))
+            nc.tensor.matmul_mx(out=t[:], lhsT=ncd[i, h // 2][:, cols].bitcast(FP8X4), lhsT_scale=nsc[i, h // 2][:, cols],
+                                rhs=ukw[h][:].bitcast(FP8X4), rhs_scale=uks[4 * h:P, :], start=True, stop=True)
+            lacc[i, h] = t
+
+        def gain_lat(i, h):
+            if h % 2 == 0:
+                t = work.tile([P, 2, R], F32, name="lat", bufs=4)
+                lat[i, h // 2] = t
+            nc.vector.tensor_tensor(out=lat[i, h // 2][:, h % 2, :], in0=lacc[i, h][:], in1=gkv[:], op=ALU.mult)
+            if h % 2 == 1:
+                nc.sync.dma_start(out=lat_out[h - 1:h + 1, i * P:(i + 1) * P, :].rearrange("h p r -> p h r"),
+                                  in_=lat[i, h // 2][:])
+
+        def rope(i):
+            part = y[i][:].rearrange("p (h c) -> p h c", h=H)
+            m1 = work.tile([P, H, E], F32, name="m1")
+            m2 = work.tile([P, H, E], F32, name="m2")
+
+            def table(t, a, b):
+                return t[:, i, a:b].unsqueeze(1).to_broadcast([P, H, b - a])
+
+            nc.gpsimd.tensor_tensor(out=m1[:], in0=part[:, :, D:HEAD], in1=table(t1, 0, E), op=ALU.mult)
+            nc.gpsimd.tensor_tensor(out=m2[:, :, 0:HALF], in0=part[:, :, D + HALF:HEAD], in1=table(t2, 0, HALF), op=ALU.mult)
+            nc.gpsimd.tensor_tensor(out=m2[:, :, HALF:E], in0=part[:, :, D:D + HALF], in1=table(t2, HALF, E), op=ALU.mult)
+            t = work.tile([P, H, E], F32, name="rsum")
+            nc.gpsimd.tensor_tensor(out=t[:], in0=m1[:], in1=m2[:], op=ALU.add)
+            rsum[i] = t
+
+        def rope_out(i):
+            t = work.tile([P, H, E], F32, name="rot")
+            for h in range(H):
+                nc.scalar.activation(out=t[:, h, :], in_=rsum[i][:, h, :], func=ACT.Copy, scale=rinv[i][:, h:h + 1])
+            nc.sync.dma_start(out=rot_out[:, i * P:(i + 1) * P, :].rearrange("h p e -> p h e"), in_=t[:])
+
+        cast(0)
+        x_turn(0)
+        x_scale(0)
+        x_quant(0)
+        cast(1)
+        for i in range(TILES + 1):
+            now, nxt, old = i < TILES, i + 1 < TILES, i > 0
+            if old:
+                for h in range(S_HEADS):
+                    norm_s(i - 1, h)
+                rope(i - 1)
+            if now:
+                up(i, 0)
+                add_bias(i, 0)
+            if old:
+                for h in range(S_HEADS, H):
+                    norm_v(i - 1, h)
+            if now:
+                gain_nope(i, 0)
+                up(i, 1)
+                add_bias(i, 1)
+                square(i, 0)
+            if nxt:
+                x_turn(i + 1)
+                x_scale(i + 1)
+            if i + 2 < TILES:
+                cast(i + 2)
+            if now:
+                up(i, 2)
+                add_bias(i, 2)
+                gain_nope(i, 1)
+                square(i, 1)
+            if nxt:
+                x_quant(i + 1)
+            if now:
+                up(i, 3)
+                add_bias(i, 3)
+                gain_nope(i, 2)
+            if old:
+                nope_turn(i - 1, 0)
+                nope_turn(i - 1, 1)
+                nope_out(i - 1, 0)
+                nope_out(i - 1, 1)
+            if now:
+                up(i, 4)
+                add_bias(i, 4)
+                square(i, 2)
+            if old:
+                nope_quant(i - 1, 0)
+                nope_quant(i - 1, 1)
+                for h in range(H):
+                    absorb(i - 1, h)
+                    gain_lat(i - 1, h)
+                rope_out(i - 1)
+            if now:
+                square(i, 3)
+                root(i)

@@ -25,7 +25,59 @@ WIDTH = H * HEAD
 BANK = 512
 BANKS = WIDTH // BANK
 HALF = E // 2
-S_HEADS = 3
+TURN_BUFS = 3
+CHUNKS = (1, 2, 2)
+
+ROUND = (
+    ("add_bias", (0,), 0),
+    ("up", (1,), 0),
+    ("x_quant", (2, 3), -1),
+    ("absorb", (3,), 3),
+    ("up", (2,), 0),
+    ("up", (3,), 0),
+    ("add_bias", (1,), 0),
+    ("up", (4,), 0),
+    ("absorb", (0,), 3),
+    ("cast", (), -2),
+    ("gain_lat", (3,), 3),
+    ("norm_s", (1,), 1),
+    ("norm_s", (0,), 1),
+    ("rope_out", (), 3),
+    ("nope_quant", (0, 4), 2),
+    ("x_turn", (2, 3), -2),
+    ("add_bias", (2,), 0),
+    ("gain_nope", (0,), 0),
+    ("square", (0,), 0),
+    ("rope", (1,), 2),
+    ("square", (1,), 0),
+    ("x_quant", (0, 2), -1),
+    ("add_bias", (3,), 0),
+    ("x_turn", (0, 2), -2),
+    ("gain_nope", (1,), 0),
+    ("absorb", (1,), 2),
+    ("norm_s", (2,), 1),
+    ("add_bias", (4,), 0),
+    ("square", (2,), 0),
+    ("absorb", (2,), 2),
+    ("rope", (2,), 2),
+    ("rope", (3,), 2),
+    ("norm_v", (3,), 1),
+    ("gain_lat", (0,), 3),
+    ("x_scale", (2,), -2),
+    ("x_scale", (1,), -2),
+    ("gain_nope", (2,), 0),
+    ("rope", (0,), 0),
+    ("gain_lat", (1,), 2),
+    ("square", (3,), 0),
+    ("up", (0,), -1),
+    ("gain_lat", (2,), 2),
+    ("nope_turn", (0,), 1),
+    ("nope_out", (0,), 1),
+    ("x_scale", (0,), -2),
+    ("nope_turn", (1,), 1),
+    ("root", (), 0),
+    ("nope_out", (1,), 1),
+)
 
 
 def tile_mla_absorbed_query_f7_kernel(tc, c_q_bytes, c_q_scale, uq_words, uq_scales, b_q, g_nope, g_rope,
@@ -39,14 +91,15 @@ def tile_mla_absorbed_query_f7_kernel(tc, c_q_bytes, c_q_scale, uq_words, uq_sca
 
         xb = [keep.tile([P, K], U8, name="xb%d" % i) for i in range(TILES)]
         cs = keep.tile([P, PASSES, 4], F32, name="cs")
-        uqw = [keep.tile([P, PASSES, 2 * BANK], U8, name="uqw%d" % b, align_bytes=64) for b in range(BANKS)]
+        uqw = [keep.tile([P, PASSES, 2 * BANK * n], U8, name="uqw%d" % j, align_bytes=64) for j, n in enumerate(CHUNKS)]
         uqs = keep.tile([P, PASSES, WIDTH], U8, name="uqs", align_bytes=64)
         ukw = [keep.tile([P, 4 * R], U8, name="ukw%d" % h, align_bytes=64) for h in range(H)]
         uks = keep.tile([P, R], U8, name="uks", align_bytes=64)
-        bias = keep.tile([P, WIDTH], BF16, name="bias")
-        gn = keep.tile([P, D], BF16, name="gn")
-        gr = keep.tile([P, E], BF16, name="gr")
-        gkv = keep.tile([P, R], BF16, name="gkv")
+        rows = keep.tile([P, WIDTH + D + R + E], BF16, name="rows")
+        ones = keep.tile([P, P], BF16, name="ones")
+        spread = keep.tile([P, WIDTH + D + R + E], F32, name="spread")
+        bias, gn = spread[:, 0:WIDTH], spread[:, WIDTH:WIDTH + D]
+        gkv, gr = spread[:, WIDTH + D:WIDTH + D + R], spread[:, WIDTH + D + R:WIDTH + D + R + E]
         cos = keep.tile([P, TILES, HALF], BF16, name="cos")
         sin = keep.tile([P, TILES, HALF], BF16, name="sin")
         t1 = keep.tile([P, TILES, E], F32, name="t1")
@@ -54,35 +107,38 @@ def tile_mla_absorbed_query_f7_kernel(tc, c_q_bytes, c_q_scale, uq_words, uq_sca
         ngr = keep.tile([P, HALF], F32, name="ngr")
         ident = keep.tile([P, P], F32, name="ident")
         warm = keep.tile([P, 1], F32, name="warm")
+        x_rows = c_q_bytes.rearrange("(p i) k -> p i k", i=TILES)
+        lat_rows = lat_out.rearrange("h (p i) r -> h p i r", i=TILES)
+        rot_rows = rot_out.rearrange("h (p i) e -> p i h e", i=TILES)
 
         def load_x(i):
-            nc.sync.dma_start(out=xb[i][:], in_=c_q_bytes[i * P:(i + 1) * P, :])
+            nc.sync.dma_start(out=xb[i][:], in_=x_rows[:, i, :])
 
+        def load_uq(j):
+            b = sum(CHUNKS[:j])
+            nc.sync.dma_start(out=uqw[j][:], in_=uq_words[:, :, 2 * BANK * b:2 * BANK * (b + CHUNKS[j])].rearrange("g p n -> p g n"))
+
+        load_x(0)
         nc.vector.memset(uqs[:].rearrange("p g n -> p (g n)").bitcast(I32), 0)
-        nc.vector.memset(uks[:].bitcast(I32), 0)
         nc.vector.memset(warm[:], 1.0)
+        nc.vector.memset(ones[:], 1.0)
+        nc.vector.memset(uks[:].bitcast(I32), 0)
+        nc.gpsimd.memset(rows[:].bitcast(F32), 0.0)
         nc.scalar.dma_start(out=cs[:], in_=c_q_scale.rearrange("o (g p t) -> p (o g) t", p=P, t=4))
         nc.scalar.activation(out=warm[:], in_=warm[:], func=ACT.Abs_reciprocal_sqrt)
         make_identity(nc, ident[:])
-        load_x(0)
-        load_x(1)
+        for vec, at in ((b_q, 0), (g_nope, WIDTH), (g_rope, WIDTH + D + R), (g_kv, WIDTH + D)):
+            n = vec.shape[0]
+            nc.scalar.dma_start(out=rows[0:1, at:at + n], in_=vec.rearrange("(o n) -> o n", o=1))
         for q in range(4):
             nc.sync.dma_start(out=uqs[32 * q:32 * q + 4, :, :].bitcast(I32),
                               in_=uq_scales[:, 4 * q:4 * q + 4, :].rearrange("g r n -> r g n").bitcast(I32))
-
-        def load_uq(b):
-            nc.sync.dma_start(out=uqw[b][:],
-                              in_=uq_words[:, :, 2 * BANK * b:2 * BANK * (b + 1)].rearrange("g p n -> p g n"))
-
         load_uq(0)
-        nc.sync.dma_start(out=bias[:], in_=b_q.partition_broadcast(P))
-        load_uq(1)
-        nc.sync.dma_start(out=gn[:], in_=g_nope.partition_broadcast(P))
-        for b in range(2, BANKS):
-            load_uq(b)
-        nc.scalar.dma_start(out=gr[:], in_=g_rope.partition_broadcast(P))
-        nc.scalar.dma_start(out=cos[:], in_=rot_cos.rearrange("(i p) j -> p i j", p=P))
-        nc.scalar.dma_start(out=sin[:], in_=rot_sin.rearrange("(i p) j -> p i j", p=P))
+        load_x(1)
+        for j in range(1, len(CHUNKS)):
+            load_uq(j)
+        nc.sync.dma_start(out=cos[:], in_=rot_cos.rearrange("(p i) j -> p i j", i=TILES))
+        nc.sync.dma_start(out=sin[:], in_=rot_sin.rearrange("(p i) j -> p i j", i=TILES))
         load_x(2)
         for q in range(4):
             nc.sync.dma_start(out=uks[32 * q:32 * q + 16, :].bitcast(I32),
@@ -90,89 +146,103 @@ def tile_mla_absorbed_query_f7_kernel(tc, c_q_bytes, c_q_scale, uq_words, uq_sca
         for h in range(H):
             nc.sync.dma_start(out=ukw[h][:].bitcast(I32),
                               in_=uk_words[h].rearrange("p n t -> p (n t)").bitcast(I32))
-        nc.sync.dma_start(out=gkv[:], in_=g_kv.partition_broadcast(P))
         for i in range(3, TILES):
             load_x(i)
 
-        def gain(col):
-            return gr[:, col:col + HALF].unsqueeze(1).to_broadcast([P, TILES, HALF])
+        def make_tables():
+            def gain(col):
+                return gr[:, col:col + HALF].unsqueeze(1).to_broadcast([P, TILES, HALF])
 
-        nc.gpsimd.tensor_scalar(out=ngr[:], in0=gr[:, HALF:E], scalar1=-1.0, scalar2=None, op0=ALU.mult)
-        nc.gpsimd.tensor_tensor(out=t1[:, :, 0:HALF], in0=cos[:], in1=gain(0), op=ALU.mult)
-        nc.gpsimd.tensor_tensor(out=t1[:, :, HALF:E], in0=cos[:], in1=gain(HALF), op=ALU.mult)
-        nc.gpsimd.tensor_tensor(out=t2[:, :, 0:HALF], in0=sin[:],
-                                in1=ngr[:].unsqueeze(1).to_broadcast([P, TILES, HALF]), op=ALU.mult)
-        nc.gpsimd.tensor_tensor(out=t2[:, :, HALF:E], in0=sin[:], in1=gain(0), op=ALU.mult)
+            nc.gpsimd.tensor_scalar(out=ngr[:], in0=gr[:, HALF:E], scalar1=-1.0, scalar2=None, op0=ALU.mult)
+            nc.gpsimd.tensor_tensor(out=t1[:, :, 0:HALF], in0=cos[:], in1=gain(0), op=ALU.mult)
+            nc.gpsimd.tensor_tensor(out=t1[:, :, HALF:E], in0=cos[:], in1=gain(HALF), op=ALU.mult)
+            nc.gpsimd.tensor_tensor(out=t2[:, :, 0:HALF], in0=sin[:],
+                                    in1=ngr[:].unsqueeze(1).to_broadcast([P, TILES, HALF]), op=ALU.mult)
+            nc.gpsimd.tensor_tensor(out=t2[:, :, HALF:E], in0=sin[:], in1=gain(0), op=ALU.mult)
+
+        def spread_row(at, n, copy):
+            t = psum.tile([P, BANK], F32, name="acc", bufs=8 - TURN_BUFS)
+            nc.tensor.matmul(t[:, 0:n], lhsT=ones[:], rhs=rows[:, at:at + n], start=True, stop=True)
+            copy(out=spread[:, at:at + n], in_=t[:, 0:n])
 
         xw, xt, xg, xc, xs = {}, {}, {}, {}, {}
         acc, y, yg, ss, rinv, nope = {}, {}, {}, {}, {}, {}
         nt, ng, ncd, nsc = {}, {}, {}, {}
-        lacc, lat, rsum = {}, {}, {}
+        lacc, lat, rsum, ropes = {}, {}, {}, {}
+
+        def cast_first():
+            t = work.tile([P, K], BF16, name="xw", bufs=3)
+            view = xb[0][:].bitcast(FP8)
+            nc.vector.tensor_copy(out=t[:, 0:512], in_=view[:, 0:512])
+            nc.scalar.copy(out=t[:, 512:1024], in_=view[:, 512:1024])
+            nc.vector.tensor_copy(out=t[:, 1024:K], in_=view[:, 1024:K])
+            xw[0] = t
 
         def cast(i):
             t = work.tile([P, K], BF16, name="xw", bufs=3)
             nc.scalar.copy(out=t[:], in_=xb[i][:].bitcast(FP8))
             xw[i] = t
 
-        def x_turn(i):
+        def x_turn(i, a, b):
             words = xw[i][:].bitcast(F32)
-            for g in range(PASSES):
-                if g % 2 == 0:
-                    bank = psum.tile([P, 4, P], F32, name="turn", bufs=3)
+            bank = psum.tile([P, 4, P], F32, name="turn", bufs=TURN_BUFS)
+            for g in range(a, b):
                 for u in range(2):
-                    nc.tensor.transpose(bank[:, 2 * (g % 2) + u, :], words[:, 256 * g + u:256 * (g + 1):2], ident[:])
-                xt[i, g] = bank[:, 2 * (g % 2):2 * (g % 2) + 2, :]
+                    nc.tensor.transpose(bank[:, 2 * (g - a) + u, :], words[:, 256 * g + u:256 * (g + 1):2], ident[:])
+                xt[i, g] = bank[:, 2 * (g - a):2 * (g - a) + 2, :]
 
-        def x_scale(i):
-            t = work.tile([P, PASSES, 4 * P], BF16, name="xg", align_bytes=64)
-            for g in range(PASSES):
-                nc.vector.tensor_tensor(
-                    out=t[:, g, :].rearrange("p (r u e) -> p r u e", u=2, e=2),
-                    in0=xt[i, g].bitcast(BF16).rearrange("p u (r e) -> p r u e", e=2),
-                    in1=cs[:, g, :].rearrange("p (u e) -> p u e", u=2).unsqueeze(1).to_broadcast([P, P, 2, 2]),
-                    op=ALU.mult)
-            xg[i] = t
+        def x_scale(i, g):
+            if i not in xg:
+                t = work.tile([P, PASSES, 4 * P], BF16, name="xg", align_bytes=64)
+                xg[i] = t
+            nc.vector.tensor_tensor(
+                out=xg[i][:, g, :].rearrange("p (r u e) -> p r u e", u=2, e=2),
+                in0=cs[:, g, :].rearrange("p (u e) -> p u e", u=2).unsqueeze(1).to_broadcast([P, P, 2, 2]),
+                in1=xt[i, g].bitcast(BF16).rearrange("p u (r e) -> p r u e", e=2),
+                op=ALU.mult)
 
-        def x_quant(i):
-            codes = work.tile([P, PASSES, P], U32, name="xc", align_bytes=64)
-            scales = work.tile([P, PASSES, P], U8, name="xs", align_bytes=64)
-            for a, b in ((0, 2), (2, 3)):
-                nc.vector.quantize_mx(out=codes[:, a:b, :].rearrange("p g n -> p (g n)").bitcast(FP8X4),
-                                      scales=scales[:, a:b, :].rearrange("p g n -> p (g n)"),
-                                      in_=xg[i][:, a:b, :].rearrange("p g n -> p (g n)"))
-            xc[i], xs[i] = codes, scales
+        def x_quant(i, a, b):
+            if i not in xc:
+                codes = work.tile([P, PASSES, P], U32, name="xc", align_bytes=64)
+                scales = work.tile([P, PASSES, P], U8, name="xs", align_bytes=64)
+                xc[i], xs[i] = codes, scales
+            nc.vector.quantize_mx(out=xc[i][:, a:b, :].rearrange("p g n -> p (g n)").bitcast(FP8X4),
+                                  scales=xs[i][:, a:b, :].rearrange("p g n -> p (g n)"),
+                                  in_=xg[i][:, a:b, :].rearrange("p g n -> p (g n)"))
 
         def up(i, b):
-            t = psum.tile([P, BANK], F32, name="acc", bufs=5)
+            j, k = ((0, 0), (1, 0), (1, 1), (2, 0), (2, 1))[b]
+            t = psum.tile([P, BANK], F32, name="acc", bufs=8 - TURN_BUFS)
             for g in range(PASSES):
                 nc.tensor.matmul_mx(out=t[:], lhsT=xc[i][:, g, :].bitcast(FP8X4), lhsT_scale=xs[i][:, g, :],
-                                    rhs=uqw[b][:, g, :].bitcast(FP4X4), rhs_scale=uqs[:, g, BANK * b:BANK * (b + 1)],
+                                    rhs=uqw[j][:, g, 2 * BANK * k:2 * BANK * (k + 1)].bitcast(FP4X4), rhs_scale=uqs[:, g, BANK * b:BANK * (b + 1)],
                                     start=(g == 0), stop=(g == PASSES - 1))
             acc[i, b] = t
 
         def add_bias(i, b):
-            if b == 0:
+            if i not in y:
                 t = work.tile([P, WIDTH], F32, name="y", bufs=3)
                 y[i] = t
             cols = slice(BANK * b, BANK * (b + 1))
-            nc.vector.tensor_tensor(out=y[i][:, cols], in0=acc[i, b][:], in1=bias[:, cols], op=ALU.add)
+            nc.vector.tensor_tensor(out=y[i][:, cols], in0=bias[:, cols], in1=acc[i, b][:], op=ALU.add)
 
         def square(i, h):
-            if h == 0:
+            if i not in ss:
                 t = work.tile([P, H], F32, name="ss")
                 ss[i] = t
             junk = work.tile([P, HEAD], BF16, name="junk")
             nc.scalar.activation(out=junk[:], in_=y[i][:, HEAD * h:HEAD * (h + 1)], func=ACT.Square,
                                  accum_out=ss[i][:, h:h + 1])
 
-        def root(i):
-            t = work.tile([P, H], F32, name="rinv", bufs=3)
-            nc.scalar.activation(out=t[:], in_=ss[i][:], func=ACT.Abs_reciprocal_sqrt, scale=1.0 / HEAD)
-            rinv[i] = t
+        def root(i, a=0, b=H):
+            if i not in rinv:
+                t = work.tile([P, H], F32, name="rinv", bufs=3)
+                rinv[i] = t
+            nc.scalar.activation(out=rinv[i][:, a:b], in_=ss[i][:, a:b], func=ACT.Abs_reciprocal_sqrt, scale=1.0 / HEAD)
 
         def gain_nope(i, h):
             t = work.tile([P, D], F32, name="yg%d" % h)
-            nc.gpsimd.tensor_tensor(out=t[:], in0=y[i][:, HEAD * h:HEAD * h + D], in1=gn[:], op=ALU.mult)
+            nc.gpsimd.tensor_tensor(out=t[:], in0=y[i][:, HEAD * h:HEAD * h + D], in1=gn, op=ALU.mult)
             yg[i, h] = t
 
         def norm_s(i, h):
@@ -185,7 +255,7 @@ def tile_mla_absorbed_query_f7_kernel(tc, c_q_bytes, c_q_scale, uq_words, uq_sca
         def norm_v(i, h):
             t = work.tile([P, D], BF16, name="nope%d" % h)
             part = y[i][:, HEAD * h:HEAD * h + D].rearrange("p (q u e) -> p u q e", u=2, e=2)
-            gpart = gn[:].rearrange("p (q u e) -> p u q e", u=2, e=2)
+            gpart = gn.rearrange("p (q u e) -> p u q e", u=2, e=2)
             for u in range(2):
                 nc.vector.scalar_tensor_tensor(out=t[:, u * 256:(u + 1) * 256].rearrange("p (q e) -> p q e", e=2),
                                                in0=part[:, u], scalar=rinv[i][:, h:h + 1], in1=gpart[:, u],
@@ -193,7 +263,7 @@ def tile_mla_absorbed_query_f7_kernel(tc, c_q_bytes, c_q_scale, uq_words, uq_sca
             nope[i, h] = t
 
         def nope_turn(i, k):
-            bank = psum.tile([P, 4, P], F32, name="turn", bufs=3)
+            bank = psum.tile([P, 4, P], F32, name="turn", bufs=TURN_BUFS)
             for j in range(2):
                 words = nope[i, 2 * k + j][:].bitcast(F32)
                 for u in range(2):
@@ -201,108 +271,78 @@ def tile_mla_absorbed_query_f7_kernel(tc, c_q_bytes, c_q_scale, uq_words, uq_sca
             nt[i, k] = bank
 
         def nope_out(i, k):
-            t = work.tile([P, 1024], BF16, name="ng", bufs=3, align_bytes=64)
-            nc.scalar.copy(out=t[:].bitcast(F32).rearrange("p (h r u) -> p h r u", h=2, u=2),
+            if i not in ng:
+                t = work.tile([P, 4 * 512], BF16, name="ng", align_bytes=64)
+                ng[i] = t
+            nc.scalar.copy(out=ng[i][:, 1024 * k:1024 * (k + 1)].bitcast(F32).rearrange("p (h r u) -> p h r u", h=2, u=2),
                            in_=nt[i, k][:].rearrange("p (h u) r -> p h r u", h=2))
-            ng[i, k] = t
 
-        def nope_quant(i, k):
-            codes = work.tile([P, 256], U32, name="ncd", bufs=4, align_bytes=64)
-            scales = work.tile([P, 256], U8, name="nsc", bufs=4, align_bytes=64)
-            nc.vector.quantize_mx(out=codes[:].bitcast(FP8X4), scales=scales[:], in_=ng[i, k][:])
-            ncd[i, k], nsc[i, k] = codes, scales
+        def nope_quant(i, a, b):
+            if i not in ncd:
+                codes = work.tile([P, BANK], U32, name="ncd", align_bytes=64)
+                scales = work.tile([P, BANK], U8, name="nsc", align_bytes=64)
+                ncd[i], nsc[i] = codes, scales
+            nc.vector.quantize_mx(out=ncd[i][:, P * a:P * b].bitcast(FP8X4), scales=nsc[i][:, P * a:P * b],
+                                  in_=ng[i][:, 512 * a:512 * b])
 
         def absorb(i, h):
-            t = psum.tile([P, BANK], F32, name="acc", bufs=5)
-            cols = slice(P * (h % 2), P * (h % 2 + 1))
-            nc.tensor.matmul_mx(out=t[:], lhsT=ncd[i, h // 2][:, cols].bitcast(FP8X4), lhsT_scale=nsc[i, h // 2][:, cols],
+            t = psum.tile([P, BANK], F32, name="acc", bufs=8 - TURN_BUFS)
+            cols = slice(P * h, P * (h + 1))
+            nc.tensor.matmul_mx(out=t[:], lhsT=ncd[i][:, cols].bitcast(FP8X4), lhsT_scale=nsc[i][:, cols],
                                 rhs=ukw[h][:].bitcast(FP8X4), rhs_scale=uks[4 * h:P, :], start=True, stop=True)
             lacc[i, h] = t
 
         def gain_lat(i, h):
-            if h % 2 == 0:
-                t = work.tile([P, 2, R], F32, name="lat", bufs=4)
-                lat[i, h // 2] = t
-            nc.vector.tensor_tensor(out=lat[i, h // 2][:, h % 2, :], in0=lacc[i, h][:], in1=gkv[:], op=ALU.mult)
-            if h % 2 == 1:
-                nc.sync.dma_start(out=lat_out[h - 1:h + 1, i * P:(i + 1) * P, :].rearrange("h p r -> p h r"),
-                                  in_=lat[i, h // 2][:])
+            t = work.tile([P, R], F32, name="lat", bufs=8)
+            nc.vector.tensor_tensor(out=t[:], in0=gkv, in1=lacc[i, h][:], op=ALU.mult)
+            nc.sync.dma_start(out=lat_rows[h, :, i, :], in_=t[:])
 
-        def rope(i):
+        def rope(i, step):
             part = y[i][:].rearrange("p (h c) -> p h c", h=H)
-            m1 = work.tile([P, H, E], F32, name="m1")
-            m2 = work.tile([P, H, E], F32, name="m2")
 
             def table(t, a, b):
                 return t[:, i, a:b].unsqueeze(1).to_broadcast([P, H, b - a])
 
-            nc.gpsimd.tensor_tensor(out=m1[:], in0=part[:, :, D:HEAD], in1=table(t1, 0, E), op=ALU.mult)
-            nc.gpsimd.tensor_tensor(out=m2[:, :, 0:HALF], in0=part[:, :, D + HALF:HEAD], in1=table(t2, 0, HALF), op=ALU.mult)
-            nc.gpsimd.tensor_tensor(out=m2[:, :, HALF:E], in0=part[:, :, D:D + HALF], in1=table(t2, HALF, E), op=ALU.mult)
-            t = work.tile([P, H, E], F32, name="rsum")
-            nc.gpsimd.tensor_tensor(out=t[:], in0=m1[:], in1=m2[:], op=ALU.add)
-            rsum[i] = t
+            if i not in ropes:
+                m1 = work.tile([P, H, E], F32, name="m1")
+                m2 = work.tile([P, H, E], F32, name="m2")
+                ropes[i] = m1, m2
+            if step == 0:
+                nc.gpsimd.tensor_tensor(out=ropes[i][0][:], in0=part[:, :, D:HEAD], in1=table(t1, 0, E), op=ALU.mult)
+            m1, m2 = ropes[i]
+            if step == 1:
+                nc.gpsimd.tensor_tensor(out=m2[:, :, 0:HALF], in0=part[:, :, D + HALF:HEAD], in1=table(t2, 0, HALF), op=ALU.mult)
+            if step == 2:
+                nc.gpsimd.tensor_tensor(out=m2[:, :, HALF:E], in0=part[:, :, D:D + HALF], in1=table(t2, HALF, E), op=ALU.mult)
+            if step == 3:
+                t = work.tile([P, H, E], F32, name="rsum")
+                nc.gpsimd.tensor_tensor(out=t[:], in0=m1[:], in1=m2[:], op=ALU.add)
+                rsum[i] = t
 
         def rope_out(i):
             t = work.tile([P, H, E], F32, name="rot")
             for h in range(H):
                 nc.scalar.activation(out=t[:, h, :], in_=rsum[i][:, h, :], func=ACT.Copy, scale=rinv[i][:, h:h + 1])
-            nc.sync.dma_start(out=rot_out[:, i * P:(i + 1) * P, :].rearrange("h p e -> p h e"), in_=t[:])
+            nc.sync.dma_start(out=rot_rows[:, i, :, :], in_=t[:])
 
-        cast(0)
-        x_turn(0)
-        x_scale(0)
-        x_quant(0)
-        cast(1)
-        for i in range(TILES + 1):
-            now, nxt, old = i < TILES, i + 1 < TILES, i > 0
-            if old:
-                for h in range(S_HEADS):
-                    norm_s(i - 1, h)
-                rope(i - 1)
-            if now:
-                up(i, 0)
-                add_bias(i, 0)
-            if old:
-                for h in range(S_HEADS, H):
-                    norm_v(i - 1, h)
-            if now:
-                gain_nope(i, 0)
-                up(i, 1)
-                add_bias(i, 1)
-                square(i, 0)
-            if nxt:
-                x_turn(i + 1)
-                x_scale(i + 1)
-            if i + 2 < TILES:
-                cast(i + 2)
-            if now:
-                up(i, 2)
-                add_bias(i, 2)
-                gain_nope(i, 1)
-                square(i, 1)
-            if nxt:
-                x_quant(i + 1)
-            if now:
-                up(i, 3)
-                add_bias(i, 3)
-                gain_nope(i, 2)
-            if old:
-                nope_turn(i - 1, 0)
-                nope_turn(i - 1, 1)
-                nope_out(i - 1, 0)
-                nope_out(i - 1, 1)
-            if now:
-                up(i, 4)
-                add_bias(i, 4)
-                square(i, 2)
-            if old:
-                nope_quant(i - 1, 0)
-                nope_quant(i - 1, 1)
-                for h in range(H):
-                    absorb(i - 1, h)
-                    gain_lat(i - 1, h)
-                rope_out(i - 1)
-            if now:
-                square(i, 3)
-                root(i)
+        cast_first()
+        for a, b in ((0, 2), (2, 3)):
+            x_turn(0, a, b)
+        for b in range(3):
+            spread_row(BANK * b, BANK, nc.scalar.copy)
+        for g in range(PASSES):
+            x_scale(0, g)
+        for a, b in ((0, 2), (2, 3)):
+            x_quant(0, a, b)
+        for b in range(3, BANKS):
+            spread_row(BANK * b, BANK, nc.vector.tensor_copy)
+        spread_row(WIDTH, D, nc.scalar.copy)
+        spread_row(WIDTH + D + R, E, nc.scalar.copy)
+        make_tables()
+        spread_row(WIDTH + D, R, nc.scalar.copy)
+        stages = {"cast": cast, "x_turn": x_turn, "x_scale": x_scale, "x_quant": x_quant, "up": up, "add_bias": add_bias, "square": square, "root": root, "gain_nope": gain_nope, "norm_s": norm_s, "norm_v": norm_v, "nope_turn": nope_turn, "nope_out": nope_out, "nope_quant": nope_quant, "absorb": absorb, "gain_lat": gain_lat, "rope": rope, "rope_out": rope_out}
+        for step in range(-3, TILES + 4):
+            for name, part, lag in ROUND:
+                first = 1 if name in ("cast", "x_turn", "x_scale", "x_quant") else 0
+                if first <= step - lag < TILES:
+                    stages[name](step - lag, *part)

@@ -29,54 +29,51 @@ TURN_BUFS = 3
 CHUNKS = (1, 2, 2)
 
 ROUND = (
-    ("add_bias", (0,), 0),
-    ("up", (1,), 0),
-    ("x_quant", (2, 3), -1),
-    ("absorb", (3,), 3),
+    ("gain_lat", (1,), 3),
+    ("rope_out", (), 2),
+    ("norm_v", (1,), 1),
     ("up", (2,), 0),
+    ("norm_v", (2,), 1),
     ("up", (3,), 0),
-    ("add_bias", (1,), 0),
-    ("up", (4,), 0),
-    ("absorb", (0,), 3),
-    ("cast", (), -2),
-    ("gain_lat", (3,), 3),
-    ("norm_s", (1,), 1),
-    ("norm_s", (0,), 1),
-    ("rope_out", (), 3),
-    ("nope_quant", (0, 4), 2),
-    ("x_turn", (2, 3), -2),
     ("add_bias", (2,), 0),
-    ("gain_nope", (0,), 0),
-    ("square", (0,), 0),
-    ("rope", (1,), 2),
-    ("square", (1,), 0),
-    ("x_quant", (0, 2), -1),
+    ("up", (1,), -1),
+    ("x_quant", (), -2),
+    ("absorb", (2,), 3),
     ("add_bias", (3,), 0),
-    ("x_turn", (0, 2), -2),
-    ("gain_nope", (1,), 0),
-    ("absorb", (1,), 2),
-    ("norm_s", (2,), 1),
-    ("add_bias", (4,), 0),
-    ("square", (2,), 0),
-    ("absorb", (2,), 2),
-    ("rope", (2,), 2),
-    ("rope", (3,), 2),
-    ("norm_v", (3,), 1),
-    ("gain_lat", (0,), 3),
-    ("x_scale", (2,), -2),
-    ("x_scale", (1,), -2),
-    ("gain_nope", (2,), 0),
-    ("rope", (0,), 0),
-    ("gain_lat", (1,), 2),
-    ("square", (3,), 0),
+    ("rope", (1,), 0),
+    ("nope_quant", (0, 4), 2),
     ("up", (0,), -1),
-    ("gain_lat", (2,), 2),
+    ("rope", (0,), 0),
+    ("cast", (), -5),
+    ("x_turn", (2, 3), -4),
+    ("add_bias", (1,), -1),
+    ("gain_lat", (2,), 3),
+    ("norm_v", (3,), 1),
+    ("add_bias", (0,), -1),
     ("nope_turn", (0,), 1),
-    ("nope_out", (0,), 1),
-    ("x_scale", (0,), -2),
-    ("nope_turn", (1,), 1),
+    ("absorb", (0,), 2),
+    ("square", (1,), 0),
+    ("square", (2,), 0),
+    ("x_turn", (0, 2), -4),
+    ("absorb", (3,), 2),
+    ("gain_lat", (0,), 2),
+    ("x_scale", (2,), -4),
+    ("up", (4,), -1),
+    ("square", (3,), 0),
+    ("gain_lat", (3,), 2),
     ("root", (), 0),
+    ("x_scale", (0,), -4),
+    ("rope", (3,), 1),
+    ("nope_turn", (1,), 1),
+    ("x_scale", (1,), -4),
+    ("nope_out", (0,), 1),
+    ("gain_nope", (0,), -1),
+    ("square", (0,), -1),
+    ("add_bias", (4,), -1),
     ("nope_out", (1,), 1),
+    ("rope", (2,), 0),
+    ("norm_s", (0,), 0),
+    ("absorb", (1,), 2),
 )
 
 
@@ -119,6 +116,7 @@ def tile_mla_absorbed_query_f7_kernel(tc, c_q_bytes, c_q_scale, uq_words, uq_sca
             nc.sync.dma_start(out=uqw[j][:], in_=uq_words[:, :, 2 * BANK * b:2 * BANK * (b + CHUNKS[j])].rearrange("g p n -> p g n"))
 
         load_x(0)
+        load_x(1)
         nc.vector.memset(uqs[:].rearrange("p g n -> p (g n)").bitcast(I32), 0)
         nc.vector.memset(warm[:], 1.0)
         nc.vector.memset(ones[:], 1.0)
@@ -134,19 +132,19 @@ def tile_mla_absorbed_query_f7_kernel(tc, c_q_bytes, c_q_scale, uq_words, uq_sca
             nc.sync.dma_start(out=uqs[32 * q:32 * q + 4, :, :].bitcast(I32),
                               in_=uq_scales[:, 4 * q:4 * q + 4, :].rearrange("g r n -> r g n").bitcast(I32))
         load_uq(0)
-        load_x(1)
         for j in range(1, len(CHUNKS)):
             load_uq(j)
         nc.sync.dma_start(out=cos[:], in_=rot_cos.rearrange("(p i) j -> p i j", i=TILES))
         nc.sync.dma_start(out=sin[:], in_=rot_sin.rearrange("(p i) j -> p i j", i=TILES))
         load_x(2)
+        load_x(3)
         for q in range(4):
             nc.sync.dma_start(out=uks[32 * q:32 * q + 16, :].bitcast(I32),
                               in_=uk_scales[:, 4 * q:4 * q + 4, :].bitcast(I32))
         for h in range(H):
             nc.sync.dma_start(out=ukw[h][:].bitcast(I32),
                               in_=uk_words[h].rearrange("p n t -> p (n t)").bitcast(I32))
-        for i in range(3, TILES):
+        for i in range(4, TILES):
             load_x(i)
 
         def make_tables():
@@ -160,8 +158,10 @@ def tile_mla_absorbed_query_f7_kernel(tc, c_q_bytes, c_q_scale, uq_words, uq_sca
                                     in1=ngr[:].unsqueeze(1).to_broadcast([P, TILES, HALF]), op=ALU.mult)
             nc.gpsimd.tensor_tensor(out=t2[:, :, HALF:E], in0=sin[:], in1=gain(0), op=ALU.mult)
 
+        gn_bank = psum.tile([P, D], F32, name="gn_bank", bufs=1)
+
         def spread_row(at, n, copy):
-            t = psum.tile([P, BANK], F32, name="acc", bufs=8 - TURN_BUFS)
+            t = gn_bank if at == WIDTH else psum.tile([P, BANK], F32, name="acc", bufs=7 - TURN_BUFS)
             nc.tensor.matmul(t[:, 0:n], lhsT=ones[:], rhs=rows[:, at:at + n], start=True, stop=True)
             copy(out=spread[:, at:at + n], in_=t[:, 0:n])
 
@@ -169,6 +169,11 @@ def tile_mla_absorbed_query_f7_kernel(tc, c_q_bytes, c_q_scale, uq_words, uq_sca
         acc, y, yg, ss, rinv, nope = {}, {}, {}, {}, {}, {}
         nt, ng, ncd, nsc = {}, {}, {}, {}
         lacc, lat, rsum, ropes = {}, {}, {}, {}
+
+        def cast_second():
+            t = work.tile([P, K], BF16, name="xw", bufs=3)
+            nc.vector.tensor_copy(out=t[:], in_=xb[1][:].bitcast(FP8))
+            xw[1] = t
 
         def cast_first():
             t = work.tile([P, K], BF16, name="xw", bufs=3)
@@ -192,29 +197,35 @@ def tile_mla_absorbed_query_f7_kernel(tc, c_q_bytes, c_q_scale, uq_words, uq_sca
                 xt[i, g] = bank[:, 2 * (g - a):2 * (g - a) + 2, :]
 
         def x_scale(i, g):
-            if i not in xg:
-                t = work.tile([P, PASSES, 4 * P], BF16, name="xg", align_bytes=64)
-                xg[i] = t
+            if i // 2 not in xg:
+                t = work.tile([P, 2, PASSES, 4 * P], BF16, name="xg", align_bytes=64)
+                xg[i // 2] = t
             nc.vector.tensor_tensor(
-                out=xg[i][:, g, :].rearrange("p (r u e) -> p r u e", u=2, e=2),
+                out=xg[i // 2][:, i % 2, g, :].rearrange("p (r u e) -> p r u e", u=2, e=2),
                 in0=cs[:, g, :].rearrange("p (u e) -> p u e", u=2).unsqueeze(1).to_broadcast([P, P, 2, 2]),
                 in1=xt[i, g].bitcast(BF16).rearrange("p u (r e) -> p r u e", e=2),
                 op=ALU.mult)
 
-        def x_quant(i, a, b):
-            if i not in xc:
-                codes = work.tile([P, PASSES, P], U32, name="xc", align_bytes=64)
-                scales = work.tile([P, PASSES, P], U8, name="xs", align_bytes=64)
-                xc[i], xs[i] = codes, scales
-            nc.vector.quantize_mx(out=xc[i][:, a:b, :].rearrange("p g n -> p (g n)").bitcast(FP8X4),
-                                  scales=xs[i][:, a:b, :].rearrange("p g n -> p (g n)"),
-                                  in_=xg[i][:, a:b, :].rearrange("p g n -> p (g n)"))
+        def x_quant(i):
+            if i > 2 and i % 2 == 1:
+                return
+            j = i // 2
+            if j not in xc:
+                codes = work.tile([P, 2, PASSES, P], U32, name="xc", align_bytes=64)
+                scales = work.tile([P, 2, PASSES, P], U8, name="xs", align_bytes=64)
+                xc[j], xs[j] = codes, scales
+            n = PASSES * P
+            at = (0, 4 * P, 2 * n) if j > 0 else (0, 2 * P, n) if i == 0 else (n, n + 2 * P, 2 * n)
+            for a, b in ((at[0], at[1]), (at[1], at[2])):
+                nc.vector.quantize_mx(out=xc[j][:].rearrange("p i g n -> p (i g n)")[:, a:b].bitcast(FP8X4),
+                                      scales=xs[j][:].rearrange("p i g n -> p (i g n)")[:, a:b],
+                                      in_=xg[j][:].rearrange("p i g n -> p (i g n)")[:, 4 * a:4 * b])
 
         def up(i, b):
             j, k = ((0, 0), (1, 0), (1, 1), (2, 0), (2, 1))[b]
-            t = psum.tile([P, BANK], F32, name="acc", bufs=8 - TURN_BUFS)
+            t = psum.tile([P, BANK], F32, name="acc", bufs=7 - TURN_BUFS)
             for g in range(PASSES):
-                nc.tensor.matmul_mx(out=t[:], lhsT=xc[i][:, g, :].bitcast(FP8X4), lhsT_scale=xs[i][:, g, :],
+                nc.tensor.matmul_mx(out=t[:], lhsT=xc[i // 2][:, i % 2, g, :].bitcast(FP8X4), lhsT_scale=xs[i // 2][:, i % 2, g, :],
                                     rhs=uqw[j][:, g, 2 * BANK * k:2 * BANK * (k + 1)].bitcast(FP4X4), rhs_scale=uqs[:, g, BANK * b:BANK * (b + 1)],
                                     start=(g == 0), stop=(g == PASSES - 1))
             acc[i, b] = t
@@ -242,24 +253,20 @@ def tile_mla_absorbed_query_f7_kernel(tc, c_q_bytes, c_q_scale, uq_words, uq_sca
 
         def gain_nope(i, h):
             t = work.tile([P, D], F32, name="yg%d" % h)
-            nc.gpsimd.tensor_tensor(out=t[:], in0=y[i][:, HEAD * h:HEAD * h + D], in1=gn, op=ALU.mult)
+            for c in range(0, D, D // 2):
+                nc.gpsimd.tensor_tensor(out=t[:, c:c + D // 2], in0=y[i][:, HEAD * h + c:HEAD * h + c + D // 2],
+                                        in1=gn[:, c:c + D // 2], op=ALU.mult)
             yg[i, h] = t
 
         def norm_s(i, h):
             t = work.tile([P, D], BF16, name="nope%d" % h)
-            nc.scalar.activation(out=t[:].rearrange("p (u q e) -> p u q e", u=2, e=2),
-                                 in_=yg[i, h][:].rearrange("p (q u e) -> p u q e", u=2, e=2),
-                                 func=ACT.Copy, scale=rinv[i][:, h:h + 1])
+            nc.scalar.activation(out=t[:], in_=yg[i, h][:], func=ACT.Copy, scale=rinv[i][:, h:h + 1])
             nope[i, h] = t
 
         def norm_v(i, h):
             t = work.tile([P, D], BF16, name="nope%d" % h)
-            part = y[i][:, HEAD * h:HEAD * h + D].rearrange("p (q u e) -> p u q e", u=2, e=2)
-            gpart = gn.rearrange("p (q u e) -> p u q e", u=2, e=2)
-            for u in range(2):
-                nc.vector.scalar_tensor_tensor(out=t[:, u * 256:(u + 1) * 256].rearrange("p (q e) -> p q e", e=2),
-                                               in0=part[:, u], scalar=rinv[i][:, h:h + 1], in1=gpart[:, u],
-                                               op0=ALU.mult, op1=ALU.mult)
+            nc.vector.scalar_tensor_tensor(out=t[:], in0=y[i][:, HEAD * h:HEAD * h + D], scalar=rinv[i][:, h:h + 1],
+                                           in1=gn_bank[:], op0=ALU.mult, op1=ALU.mult)
             nope[i, h] = t
 
         def nope_turn(i, k):
@@ -267,7 +274,7 @@ def tile_mla_absorbed_query_f7_kernel(tc, c_q_bytes, c_q_scale, uq_words, uq_sca
             for j in range(2):
                 words = nope[i, 2 * k + j][:].bitcast(F32)
                 for u in range(2):
-                    nc.tensor.transpose(bank[:, 2 * j + u, :], words[:, P * u:P * (u + 1)], ident[:])
+                    nc.tensor.transpose(bank[:, 2 * j + u, :], words[:, u:2 * P:2], ident[:])
             nt[i, k] = bank
 
         def nope_out(i, k):
@@ -286,7 +293,7 @@ def tile_mla_absorbed_query_f7_kernel(tc, c_q_bytes, c_q_scale, uq_words, uq_sca
                                   in_=ng[i][:, 512 * a:512 * b])
 
         def absorb(i, h):
-            t = psum.tile([P, BANK], F32, name="acc", bufs=8 - TURN_BUFS)
+            t = psum.tile([P, BANK], F32, name="acc", bufs=7 - TURN_BUFS)
             cols = slice(P * h, P * (h + 1))
             nc.tensor.matmul_mx(out=t[:], lhsT=ncd[i][:, cols].bitcast(FP8X4), lhsT_scale=nsc[i][:, cols],
                                 rhs=ukw[h][:].bitcast(FP8X4), rhs_scale=uks[4 * h:P, :], start=True, stop=True)
@@ -300,15 +307,17 @@ def tile_mla_absorbed_query_f7_kernel(tc, c_q_bytes, c_q_scale, uq_words, uq_sca
         def rope(i, step):
             part = y[i][:].rearrange("p (h c) -> p h c", h=H)
 
-            def table(t, a, b):
-                return t[:, i, a:b].unsqueeze(1).to_broadcast([P, H, b - a])
+            def table(t, a, b, n=H):
+                return t[:, i, a:b].unsqueeze(1).to_broadcast([P, n, b - a])
 
             if i not in ropes:
                 m1 = work.tile([P, H, E], F32, name="m1")
                 m2 = work.tile([P, H, E], F32, name="m2")
                 ropes[i] = m1, m2
             if step == 0:
-                nc.gpsimd.tensor_tensor(out=ropes[i][0][:], in0=part[:, :, D:HEAD], in1=table(t1, 0, E), op=ALU.mult)
+                for h in (0, 2):
+                    nc.gpsimd.tensor_tensor(out=ropes[i][0][:, h:h + 2, :], in0=part[:, h:h + 2, D:HEAD],
+                                            in1=table(t1, 0, E, 2), op=ALU.mult)
             m1, m2 = ropes[i]
             if step == 1:
                 nc.gpsimd.tensor_tensor(out=m2[:, :, 0:HALF], in0=part[:, :, D + HALF:HEAD], in1=table(t2, 0, HALF), op=ALU.mult)
@@ -316,7 +325,8 @@ def tile_mla_absorbed_query_f7_kernel(tc, c_q_bytes, c_q_scale, uq_words, uq_sca
                 nc.gpsimd.tensor_tensor(out=m2[:, :, HALF:E], in0=part[:, :, D:D + HALF], in1=table(t2, HALF, E), op=ALU.mult)
             if step == 3:
                 t = work.tile([P, H, E], F32, name="rsum")
-                nc.gpsimd.tensor_tensor(out=t[:], in0=m1[:], in1=m2[:], op=ALU.add)
+                for h in (0, 2):
+                    nc.gpsimd.tensor_tensor(out=t[:, h:h + 2, :], in0=m1[:, h:h + 2, :], in1=m2[:, h:h + 2, :], op=ALU.add)
                 rsum[i] = t
 
         def rope_out(i):
@@ -332,17 +342,22 @@ def tile_mla_absorbed_query_f7_kernel(tc, c_q_bytes, c_q_scale, uq_words, uq_sca
             spread_row(BANK * b, BANK, nc.scalar.copy)
         for g in range(PASSES):
             x_scale(0, g)
+        cast_second()
+        x_quant(0)
         for a, b in ((0, 2), (2, 3)):
-            x_quant(0, a, b)
+            x_turn(1, a, b)
         for b in range(3, BANKS):
-            spread_row(BANK * b, BANK, nc.vector.tensor_copy)
+            spread_row(BANK * b, BANK, nc.scalar.copy)
+        for g in range(PASSES):
+            x_scale(1, g)
+        x_quant(1)
         spread_row(WIDTH, D, nc.scalar.copy)
         spread_row(WIDTH + D + R, E, nc.scalar.copy)
         make_tables()
         spread_row(WIDTH + D, R, nc.scalar.copy)
         stages = {"cast": cast, "x_turn": x_turn, "x_scale": x_scale, "x_quant": x_quant, "up": up, "add_bias": add_bias, "square": square, "root": root, "gain_nope": gain_nope, "norm_s": norm_s, "norm_v": norm_v, "nope_turn": nope_turn, "nope_out": nope_out, "nope_quant": nope_quant, "absorb": absorb, "gain_lat": gain_lat, "rope": rope, "rope_out": rope_out}
-        for step in range(-3, TILES + 4):
+        for step in range(-5, TILES + 4):
             for name, part, lag in ROUND:
-                first = 1 if name in ("cast", "x_turn", "x_scale", "x_quant") else 0
+                first = 2 if name in ("cast", "x_turn", "x_scale", "x_quant") else 0
                 if first <= step - lag < TILES:
                     stages[name](step - lag, *part)

from contextlib import ExitStack

import concourse.mybir as mybir
from concourse.masks import make_identity

M, K, H, D, E, R = 1024, 1536, 4, 512, 128, 512
FLOPS = 2 * M * K * H * (D + E) + 2 * H * M * D * R

F32 = mybir.dt.float32
BF16 = mybir.dt.bfloat16
U32 = mybir.dt.uint32
I32 = mybir.dt.int32
U8 = mybir.dt.uint8
FP8 = mybir.dt.float8_e4m3fn
FP8X4 = mybir.dt.float8_e4m3fn_x4
FP4X4 = mybir.dt.float4_e2m1fn_x4
ALU = mybir.AluOpType
ACT = mybir.ActivationFunctionType

P = 128
TILES = M // P
PASSES = K // 512
HEAD = D + E
WIDTH = H * HEAD
BANK = 512
BANKS = WIDTH // BANK
HALF = E // 2
TURN_BUFS = 3
CHUNKS = (1, 2, 2)

ROUND = (
    ("gain_lat", (1,), 3),
    ("rope_out", (), 2),
    ("norm_v", (1,), 1),
    ("up", (2,), 0),
    ("norm_v", (2,), 1),
    ("up", (3,), 0),
    ("add_bias", (2,), 0),
    ("up", (1,), -1),
    ("x_quant", (), -2),
    ("absorb", (2,), 3),
    ("add_bias", (3,), 0),
    ("rope", (1,), 0),
    ("nope_quant", (0, 4), 2),
    ("up", (0,), -1),
    ("rope", (0,), 0),
    ("cast", (), -5),
    ("x_turn", (2, 3), -4),
    ("add_bias", (1,), -1),
    ("gain_lat", (2,), 3),
    ("norm_v", (3,), 1),
    ("add_bias", (0,), -1),
    ("nope_turn", (0,), 1),
    ("absorb", (0,), 2),
    ("square", (1,), 0),
    ("square", (2,), 0),
    ("x_turn", (0, 2), -4),
    ("absorb", (3,), 2),
    ("gain_lat", (0,), 2),
    ("x_scale", (2,), -4),
    ("up", (4,), -1),
    ("square", (3,), 0),
    ("gain_lat", (3,), 2),
    ("root", (), 0),
    ("x_scale", (0,), -4),
    ("rope", (3,), 1),
    ("nope_turn", (1,), 1),
    ("x_scale", (1,), -4),
    ("nope_out", (0,), 1),
    ("gain_nope", (0,), -1),
    ("square", (0,), -1),
    ("add_bias", (4,), -1),
    ("nope_out", (1,), 1),
    ("rope", (2,), 0),
    ("norm_s", (0,), 0),
    ("absorb", (1,), 2),
)


def tile_mla_absorbed_query_f7_kernel(tc, c_q_bytes, c_q_scale, uq_words, uq_scales, b_q, g_nope, g_rope,
                                                  rot_cos, rot_sin, uk_words, uk_scales, g_kv, lat_out, rot_out):
    nc = tc.nc
    with ExitStack() as ctx:
        keep = ctx.enter_context(tc.tile_pool(name="keep", bufs=1))
        work = ctx.enter_context(tc.tile_pool(name="work", bufs=2))
        psum = ctx.enter_context(tc.psum_pool(name="psum", bufs=2))
        ctx.enter_context(tc.manual_schedule())

        xb = [keep.tile([P, K], U8, name="xb%d" % i) for i in range(TILES)]
        cs = keep.tile([P, PASSES, 4], F32, name="cs")
        uqw = [keep.tile([P, PASSES, 2 * BANK * n], U8, name="uqw%d" % j, align_bytes=64) for j, n in enumerate(CHUNKS)]
        uqs = keep.tile([P, PASSES, WIDTH], U8, name="uqs", align_bytes=64)
        ukw = [keep.tile([P, 4 * R], U8, name="ukw%d" % h, align_bytes=64) for h in range(H)]
        uks = keep.tile([P, R], U8, name="uks", align_bytes=64)
        rows = keep.tile([P, WIDTH + D + R + E], BF16, name="rows")
        ones = keep.tile([P, P], BF16, name="ones")
        spread = keep.tile([P, WIDTH + D + R + E], F32, name="spread")
        bias, gn = spread[:, 0:WIDTH], spread[:, WIDTH:WIDTH + D]
        gkv, gr = spread[:, WIDTH + D:WIDTH + D + R], spread[:, WIDTH + D + R:WIDTH + D + R + E]
        cos = keep.tile([P, TILES, HALF], BF16, name="cos")
        sin = keep.tile([P, TILES, HALF], BF16, name="sin")
        t1 = keep.tile([P, TILES, E], F32, name="t1")
        t2 = keep.tile([P, TILES, E], F32, name="t2")
        ngr = keep.tile([P, HALF], F32, name="ngr")
        ident = keep.tile([P, P], F32, name="ident")
        warm = keep.tile([P, 1], F32, name="warm")
        x_rows = c_q_bytes.rearrange("(p i) k -> p i k", i=TILES)
        lat_rows = lat_out.rearrange("h (p i) r -> h p i r", i=TILES)
        rot_rows = rot_out.rearrange("h (p i) e -> p i h e", i=TILES)

        def load_x(i):
            nc.sync.dma_start(out=xb[i][:], in_=x_rows[:, i, :])

        def load_uq(j):
            b = sum(CHUNKS[:j])
            nc.sync.dma_start(out=uqw[j][:], in_=uq_words[:, :, 2 * BANK * b:2 * BANK * (b + CHUNKS[j])].rearrange("g p n -> p g n"))

        load_x(0)
        load_x(1)
        nc.vector.memset(uqs[:].rearrange("p g n -> p (g n)").bitcast(I32), 0)
        nc.vector.memset(warm[:], 1.0)
        nc.vector.memset(ones[:], 1.0)
        nc.vector.memset(uks[:].bitcast(I32), 0)
        nc.gpsimd.memset(rows[:].bitcast(F32), 0.0)
        nc.scalar.dma_start(out=cs[:], in_=c_q_scale.rearrange("o (g p t) -> p (o g) t", p=P, t=4))
        nc.scalar.activation(out=warm[:], in_=warm[:], func=ACT.Abs_reciprocal_sqrt)
        make_identity(nc, ident[:])
        for vec, at in ((b_q, 0), (g_nope, WIDTH), (g_rope, WIDTH + D + R), (g_kv, WIDTH + D)):
            n = vec.shape[0]
            nc.scalar.dma_start(out=rows[0:1, at:at + n], in_=vec.rearrange("(o n) -> o n", o=1))
        for q in range(4):
            nc.sync.dma_start(out=uqs[32 * q:32 * q + 4, :, :].bitcast(I32),
                              in_=uq_scales[:, 4 * q:4 * q + 4, :].rearrange("g r n -> r g n").bitcast(I32))
        load_uq(0)
        for j in range(1, len(CHUNKS)):
            load_uq(j)
        nc.sync.dma_start(out=cos[:], in_=rot_cos.rearrange("(p i) j -> p i j", i=TILES))
        nc.sync.dma_start(out=sin[:], in_=rot_sin.rearrange("(p i) j -> p i j", i=TILES))
        load_x(2)
        load_x(3)
        for q in range(4):
            nc.sync.dma_start(out=uks[32 * q:32 * q + 16, :].bitcast(I32),
                              in_=uk_scales[:, 4 * q:4 * q + 4, :].bitcast(I32))
        for h in range(H):
            nc.sync.dma_start(out=ukw[h][:].bitcast(I32),
                              in_=uk_words[h].rearrange("p n t -> p (n t)").bitcast(I32))
        for i in range(4, TILES):
            load_x(i)

        def make_tables():
            def gain(col):
                return gr[:, col:col + HALF].unsqueeze(1).to_broadcast([P, TILES, HALF])

            nc.gpsimd.tensor_scalar(out=ngr[:], in0=gr[:, HALF:E], scalar1=-1.0, scalar2=None, op0=ALU.mult)
            nc.gpsimd.tensor_tensor(out=t1[:, :, 0:HALF], in0=cos[:], in1=gain(0), op=ALU.mult)
            nc.gpsimd.tensor_tensor(out=t1[:, :, HALF:E], in0=cos[:], in1=gain(HALF), op=ALU.mult)
            nc.gpsimd.tensor_tensor(out=t2[:, :, 0:HALF], in0=sin[:],
                                    in1=ngr[:].unsqueeze(1).to_broadcast([P, TILES, HALF]), op=ALU.mult)
            nc.gpsimd.tensor_tensor(out=t2[:, :, HALF:E], in0=sin[:], in1=gain(0), op=ALU.mult)

        gn_bank = psum.tile([P, D], F32, name="gn_bank", bufs=1)

        def spread_row(at, n, copy):
            t = gn_bank if at == WIDTH else psum.tile([P, BANK], F32, name="acc", bufs=7 - TURN_BUFS)
            nc.tensor.matmul(t[:, 0:n], lhsT=ones[:], rhs=rows[:, at:at + n], start=True, stop=True)
            copy(out=spread[:, at:at + n], in_=t[:, 0:n])

        xw, xt, xg, xc, xs = {}, {}, {}, {}, {}
        acc, y, yg, ss, rinv, nope = {}, {}, {}, {}, {}, {}
        nt, ng, ncd, nsc = {}, {}, {}, {}
        lacc, lat, rsum, ropes = {}, {}, {}, {}

        def cast_second():
            t = work.tile([P, K], BF16, name="xw", bufs=3)
            nc.vector.tensor_copy(out=t[:], in_=xb[1][:].bitcast(FP8))
            xw[1] = t

        def cast_first():
            t = work.tile([P, K], BF16, name="xw", bufs=3)
            view = xb[0][:].bitcast(FP8)
            nc.vector.tensor_copy(out=t[:, 0:512], in_=view[:, 0:512])
            nc.scalar.copy(out=t[:, 512:1024], in_=view[:, 512:1024])
            nc.vector.tensor_copy(out=t[:, 1024:K], in_=view[:, 1024:K])
            xw[0] = t

        def cast(i):
            t = work.tile([P, K], BF16, name="xw", bufs=3)
            nc.scalar.copy(out=t[:], in_=xb[i][:].bitcast(FP8))
            xw[i] = t

        def x_turn(i, a, b):
            words = xw[i][:].bitcast(F32)
            bank = psum.tile([P, 4, P], F32, name="turn", bufs=TURN_BUFS)
            for g in range(a, b):
                for u in range(2):
                    nc.tensor.transpose(bank[:, 2 * (g - a) + u, :], words[:, 256 * g + u:256 * (g + 1):2], ident[:])
                xt[i, g] = bank[:, 2 * (g - a):2 * (g - a) + 2, :]

        def x_scale(i, g):
            if i // 2 not in xg:
                t = work.tile([P, 2, PASSES, 4 * P], BF16, name="xg", align_bytes=64)
                xg[i // 2] = t
            nc.vector.tensor_tensor(
                out=xg[i // 2][:, i % 2, g, :].rearrange("p (r u e) -> p r u e", u=2, e=2),
                in0=cs[:, g, :].rearrange("p (u e) -> p u e", u=2).unsqueeze(1).to_broadcast([P, P, 2, 2]),
                in1=xt[i, g].bitcast(BF16).rearrange("p u (r e) -> p r u e", e=2),
                op=ALU.mult)

        def x_quant(i):
            if i > 2 and i % 2 == 1:
                return
            j = i // 2
            if j not in xc:
                codes = work.tile([P, 2, PASSES, P], U32, name="xc", align_bytes=64)
                scales = work.tile([P, 2, PASSES, P], U8, name="xs", align_bytes=64)
                xc[j], xs[j] = codes, scales
            n = PASSES * P
            at = (0, 4 * P, 2 * n) if j > 0 else (0, 2 * P, n) if i == 0 else (n, n + 2 * P, 2 * n)
            for a, b in ((at[0], at[1]), (at[1], at[2])):
                nc.vector.quantize_mx(out=xc[j][:].rearrange("p i g n -> p (i g n)")[:, a:b].bitcast(FP8X4),
                                      scales=xs[j][:].rearrange("p i g n -> p (i g n)")[:, a:b],
                                      in_=xg[j][:].rearrange("p i g n -> p (i g n)")[:, 4 * a:4 * b])

        def up(i, b):
            j, k = ((0, 0), (1, 0), (1, 1), (2, 0), (2, 1))[b]
            t = psum.tile([P, BANK], F32, name="acc", bufs=7 - TURN_BUFS)
            for g in range(PASSES):
                nc.tensor.matmul_mx(out=t[:], lhsT=xc[i // 2][:, i % 2, g, :].bitcast(FP8X4), lhsT_scale=xs[i // 2][:, i % 2, g, :],
                                    rhs=uqw[j][:, g, 2 * BANK * k:2 * BANK * (k + 1)].bitcast(FP4X4), rhs_scale=uqs[:, g, BANK * b:BANK * (b + 1)],
                                    start=(g == 0), stop=(g == PASSES - 1))
            acc[i, b] = t

        def add_bias(i, b):
            if i not in y:
                t = work.tile([P, WIDTH], F32, name="y", bufs=3)
                y[i] = t
            cols = slice(BANK * b, BANK * (b + 1))
            nc.vector.tensor_tensor(out=y[i][:, cols], in0=bias[:, cols], in1=acc[i, b][:], op=ALU.add)

        def square(i, h):
            if i not in ss:
                t = work.tile([P, H], F32, name="ss")
                ss[i] = t
            junk = work.tile([P, HEAD], BF16, name="junk")
            nc.scalar.activation(out=junk[:], in_=y[i][:, HEAD * h:HEAD * (h + 1)], func=ACT.Square,
                                 accum_out=ss[i][:, h:h + 1])

        def root(i, a=0, b=H):
            if i not in rinv:
                t = work.tile([P, H], F32, name="rinv", bufs=3)
                rinv[i] = t
            nc.scalar.activation(out=rinv[i][:, a:b], in_=ss[i][:, a:b], func=ACT.Abs_reciprocal_sqrt, scale=1.0 / HEAD)

        def gain_nope(i, h):
            t = work.tile([P, D], F32, name="yg%d" % h)
            for c in range(0, D, D // 2):
                nc.gpsimd.tensor_tensor(out=t[:, c:c + D // 2], in0=y[i][:, HEAD * h + c:HEAD * h + c + D // 2],
                                        in1=gn[:, c:c + D // 2], op=ALU.mult)
            yg[i, h] = t

        def norm_s(i, h):
            t = work.tile([P, D], BF16, name="nope%d" % h)
            nc.scalar.activation(out=t[:], in_=yg[i, h][:], func=ACT.Copy, scale=rinv[i][:, h:h + 1])
            nope[i, h] = t

        def norm_v(i, h):
            t = work.tile([P, D], BF16, name="nope%d" % h)
            nc.vector.scalar_tensor_tensor(out=t[:], in0=y[i][:, HEAD * h:HEAD * h + D], scalar=rinv[i][:, h:h + 1],
                                           in1=gn_bank[:], op0=ALU.mult, op1=ALU.mult)
            nope[i, h] = t

        def nope_turn(i, k):
            bank = psum.tile([P, 4, P], F32, name="turn", bufs=TURN_BUFS)
            for j in range(2):
                words = nope[i, 2 * k + j][:].bitcast(F32)
                for u in range(2):
                    nc.tensor.transpose(bank[:, 2 * j + u, :], words[:, u:2 * P:2], ident[:])
            nt[i, k] = bank

        def nope_out(i, k):
            if i not in ng:
                t = work.tile([P, 4 * 512], BF16, name="ng", align_bytes=64)
                ng[i] = t
            nc.scalar.copy(out=ng[i][:, 1024 * k:1024 * (k + 1)].bitcast(F32).rearrange("p (h r u) -> p h r u", h=2, u=2),
                           in_=nt[i, k][:].rearrange("p (h u) r -> p h r u", h=2))

        def nope_quant(i, a, b):
            if i not in ncd:
                codes = work.tile([P, BANK], U32, name="ncd", align_bytes=64)
                scales = work.tile([P, BANK], U8, name="nsc", align_bytes=64)
                ncd[i], nsc[i] = codes, scales
            nc.vector.quantize_mx(out=ncd[i][:, P * a:P * b].bitcast(FP8X4), scales=nsc[i][:, P * a:P * b],
                                  in_=ng[i][:, 512 * a:512 * b])

        def absorb(i, h):
            t = psum.tile([P, BANK], F32, name="acc", bufs=7 - TURN_BUFS)
            cols = slice(P * h, P * (h + 1))
            nc.tensor.matmul_mx(out=t[:], lhsT=ncd[i][:, cols].bitcast(FP8X4), lhsT_scale=nsc[i][:, cols],
                                rhs=ukw[h][:].bitcast(FP8X4), rhs_scale=uks[4 * h:P, :], start=True, stop=True)
            lacc[i, h] = t

        def gain_lat(i, h):
            t = work.tile([P, R], F32, name="lat", bufs=8)
            nc.vector.tensor_tensor(out=t[:], in0=gkv, in1=lacc[i, h][:], op=ALU.mult)
            nc.sync.dma_start(out=lat_rows[h, :, i, :], in_=t[:])

        def rope(i, step):
            part = y[i][:].rearrange("p (h c) -> p h c", h=H)

            def table(t, a, b, n=H):
                return t[:, i, a:b].unsqueeze(1).to_broadcast([P, n, b - a])

            if i not in ropes:
                m1 = work.tile([P, H, E], F32, name="m1")
                m2 = work.tile([P, H, E], F32, name="m2")
                ropes[i] = m1, m2
            if step == 0:
                for h in (0, 2):
                    nc.gpsimd.tensor_tensor(out=ropes[i][0][:, h:h + 2, :], in0=part[:, h:h + 2, D:HEAD],
                                            in1=table(t1, 0, E, 2), op=ALU.mult)
            m1, m2 = ropes[i]
            if step == 1:
                nc.gpsimd.tensor_tensor(out=m2[:, :, 0:HALF], in0=part[:, :, D + HALF:HEAD], in1=table(t2, 0, HALF), op=ALU.mult)
            if step == 2:
                nc.gpsimd.tensor_tensor(out=m2[:, :, HALF:E], in0=part[:, :, D:D + HALF], in1=table(t2, HALF, E), op=ALU.mult)
            if step == 3:
                t = work.tile([P, H, E], F32, name="rsum")
                for h in (0, 2):
                    nc.gpsimd.tensor_tensor(out=t[:, h:h + 2, :], in0=m1[:, h:h + 2, :], in1=m2[:, h:h + 2, :], op=ALU.add)
                rsum[i] = t

        def rope_out(i):
            t = work.tile([P, H, E], F32, name="rot")
            for h in range(H):
                nc.scalar.activation(out=t[:, h, :], in_=rsum[i][:, h, :], func=ACT.Copy, scale=rinv[i][:, h:h + 1])
            nc.sync.dma_start(out=rot_rows[:, i, :, :], in_=t[:])

        cast_first()
        for a, b in ((0, 2), (2, 3)):
            x_turn(0, a, b)
        for b in range(3):
            spread_row(BANK * b, BANK, nc.scalar.copy)
        for g in range(PASSES):
            x_scale(0, g)
        cast_second()
        x_quant(0)
        for a, b in ((0, 2), (2, 3)):
            x_turn(1, a, b)
        for b in range(3, BANKS):
            spread_row(BANK * b, BANK, nc.scalar.copy)
        for g in range(PASSES):
            x_scale(1, g)
        x_quant(1)
        spread_row(WIDTH, D, nc.scalar.copy)
        spread_row(WIDTH + D + R, E, nc.scalar.copy)
        make_tables()
        spread_row(WIDTH + D, R, nc.scalar.copy)
        stages = {"cast": cast, "x_turn": x_turn, "x_scale": x_scale, "x_quant": x_quant, "up": up, "add_bias": add_bias, "square": square, "root": root, "gain_nope": gain_nope, "norm_s": norm_s, "norm_v": norm_v, "nope_turn": nope_turn, "nope_out": nope_out, "nope_quant": nope_quant, "absorb": absorb, "gain_lat": gain_lat, "rope": rope, "rope_out": rope_out}
        for step in range(-5, TILES + 4):
            for name, part, lag in ROUND:
                first = 2 if name in ("cast", "x_turn", "x_scale", "x_quant") else 0
                if first <= step - lag < TILES:
                    stages[name](step - lag, *part)
